import numpy as np
import ml_dtypes


def mxq(x, axis, fmt="e4m3"):
    dtype, down = {"e4m3": (ml_dtypes.float8_e4m3fn, 7), "e5m2": (ml_dtypes.float8_e5m2, 14)}[fmt]
    v = np.moveaxis(np.asarray(x, np.float32).astype(ml_dtypes.bfloat16).astype(np.float64), axis, -1)
    blocks = v.reshape(v.shape[:-1] + (-1, 32))
    amax = np.abs(blocks).max(-1, keepdims=True)
    byte = np.maximum(np.where(amax > 0, np.frexp(amax)[1] - 1 + 127, 0) - down, 1)
    scale = np.exp2(byte - 127.0)
    codes = (blocks / scale).astype(np.float32).astype(dtype).astype(np.float64)
    return np.moveaxis((codes * scale).reshape(v.shape), -1, axis)


WIDE = False


def mx_kscale(k):
    if not WIDE:
        return np.ones(k)
    levels = np.array([10, -10, 5, -5, 0])
    if k % 512:
        return np.exp2(np.random.permutation(np.resize(levels, k // 32))).repeat(32)
    a = np.empty((k // 512, 16))
    for p in range(k // 512):
        a[p, :8] = np.random.permutation(np.resize(levels, 8))
        for g in range(8):
            far = levels[np.abs(levels - a[p, g]) >= 10]
            a[p, g + 8] = far[np.random.randint(len(far))]
    return np.exp2(a.ravel()).repeat(32)


def f64(x):
    return np.asarray(x).astype(np.float64)


E2M1 = np.array([0.0, 0.5, 1.0, 1.5, 2.0, 3.0, 4.0, 6.0, -0.0, -0.5, -1.0, -1.5, -2.0, -3.0, -4.0, -6.0])


def pack_weight(w, fmt):
    k, n = w.shape
    w = f64(np.asarray(w, np.float32).astype(ml_dtypes.bfloat16)).reshape(k // 32, 32, n)
    amax = np.abs(w).max(1)
    if fmt == "e4m3":
        byte = np.frexp(amax)[1] - 1 + 127 - 7
    else:
        mant, ex = np.frexp(amax / 6.0)
        byte = np.where(mant > 0.5, ex, ex - 1) + 127
    byte = np.clip(np.where(amax > 0, byte, 1), 1, 254)
    scaled = (w * np.exp2(127.0 - byte)[:, None, :]).reshape(k, n).astype(np.float32)
    by_word = np.ascontiguousarray(scaled.reshape(k // 512, 128, 4, n).transpose(0, 1, 3, 2))
    if fmt == "e4m3":
        words = by_word.astype(ml_dtypes.float8_e4m3fn).view(np.uint8)
    else:
        c = by_word.astype(ml_dtypes.float4_e2m1fn).view(np.uint8) & 0xF
        words = (c[..., 0::2] | (c[..., 1::2] << 4)).reshape(k // 512, 128, 2 * n)
    return np.ascontiguousarray(words), np.ascontiguousarray(byte.astype(np.uint8).reshape(k // 512, 16, n))


def unpack_weight(words, scales, fmt):
    g, _, n = scales.shape
    words = np.ascontiguousarray(words).reshape(g, 128, n, -1)
    if fmt == "e4m3":
        vals = words.view(ml_dtypes.float8_e4m3fn).astype(np.float64)
    else:
        nib = np.empty((g, 128, n, 4), np.uint8)
        nib[..., 0::2] = words & 0xF
        nib[..., 1::2] = words >> 4
        vals = E2M1[nib]
    vals = vals * np.repeat(np.exp2(scales.astype(np.float64) - 127.0), 8, axis=1)[..., None]
    return vals.transpose(0, 1, 3, 2).reshape(g * 512, n)


def silu(v):
    return v / (1.0 + np.exp(-np.maximum(v, -700.0)))


K, M, T = 1536, 1536, 512


def setup_inputs():
    n = np.random.standard_normal
    s = mx_kscale(K)[:, None]
    p_w4 = pack_weight(n((K, M)) / np.sqrt(K) / s, "e2m1")
    p_w8 = pack_weight(n((K, M)) / np.sqrt(K) / s, "e4m3")
    return {
        "x": (n((K, T)) * s).astype(np.float32),
        "w4_words": p_w4[0],
        "w4_scales": p_w4[1],
        "w8_words": p_w8[0],
        "w8_scales": p_w8[1],
        "r": (n((1536, 512))).astype(np.float32),
    }


def reference(x, w4_words, w4_scales, w8_words, w8_scales, r):
    x_ = mxq(f64(x), 0, "e4m3")
    w4_ = unpack_weight(w4_words, w4_scales, "e2m1")
    w8_ = unpack_weight(w8_words, w8_scales, "e4m3")
    y = w4_.T @ x_
    u = w8_.T @ x_
    y = silu(y) * u
    return f64(r) + y

@@ -1,0 +1,196 @@
+from contextlib import ExitStack
+
+import concourse.mybir as mybir
+
+K, M, T = 1536, 1536, 512
+FLOPS = 2 * 2 * K * M * T
+
+F32 = mybir.dt.float32
+BF16 = mybir.dt.bfloat16
+I32 = mybir.dt.int32
+U32 = mybir.dt.uint32
+U8 = mybir.dt.uint8
+FP8X4 = mybir.dt.float8_e4m3fn_x4
+FP4X4 = mybir.dt.float4_e2m1fn_x4
+ACT = mybir.ActivationFunctionType
+ALU = mybir.AluOpType
+
+P = 128
+PACK = 4
+KP = P * PACK
+NP = K // KP
+NT = M // P
+C0 = 512
+SPLIT = 320
+
+
+def tile_mix_glu48_fm_res_kernel(tc, x, w4_words, w4_scales, w8_words, w8_scales, r, out):
+    nc = tc.nc
+    w8_rows = w8_words.rearrange("a p n i -> a p (n i)")
+    r_rows = r.rearrange("(i p) t -> p i t", p=P)
+    out_rows = out.rearrange("(i p) t -> p i t", p=P)
+
+    with ExitStack() as ctx:
+        keep = ctx.enter_context(tc.tile_pool(name="keep", bufs=1))
+        work = ctx.enter_context(tc.tile_pool(name="work", bufs=4))
+        psum = ctx.enter_context(tc.psum_pool(name="psum", bufs=1))
+        ctx.enter_context(tc.manual_schedule())
+
+        w8 = keep.tile([P, NP, M], U32, name="w8", align_bytes=256)
+        w4 = keep.tile([P, NP, 2 * M], U8, name="w4", align_bytes=256)
+        s8 = keep.tile([P, M], U8, name="s8", align_bytes=256)
+        s4 = keep.tile([P, NP, M], U8, name="s4", align_bytes=256)
+        xc = keep.tile([P, NP, T], U32, name="xc", align_bytes=256)
+        xs = keep.tile([P, NP, T], U8, name="xs", align_bytes=256)
+        res = keep.tile([P, NT, T], F32, name="res", align_bytes=256)
+        xf = [keep.tile([P, PACK, T], F32, name="xf%d" % a, align_bytes=256) for a in range(NP)]
+        xb = [keep.tile([P, T, PACK], BF16, name="xb%d" % a, align_bytes=256) for a in range(NP)]
+        one = keep.tile([P, 1], F32, name="one")
+        junk = keep.tile([P, 1], F32, name="junk")
+
+        nc.vector.memset(s8[:].bitcast(U32), 0)
+        nc.vector.memset(s4[:].rearrange("p a n -> p (a n)").bitcast(U32), 0)
+        nc.vector.memset(one[:], 0.0)
+
+        def load_x(a):
+            nc.sync.dma_start(out=xf[a][:], in_=x[a * KP : (a + 1) * KP, :].rearrange("(p j) t -> p j t", j=PACK))
+
+        def load_w8(a0, a1, c0, c1):
+            for_a = w8_rows[a0:a1, :, 4 * c0 : 4 * c1].bitcast(I32).rearrange("a p n -> p a n")
+            nc.sync.dma_start(out=w8[:, a0:a1, c0:c1].bitcast(I32), in_=for_a)
+
+        def load_w4(a0, a1, c0, c1):
+            for_a = w4_words[a0:a1, :, 2 * c0 : 2 * c1].bitcast(I32).rearrange("a p n -> p a n")
+            nc.sync.dma_start(out=w4[:, a0:a1, 2 * c0 : 2 * c1].bitcast(I32), in_=for_a)
+
+        def load_r(i0, i1):
+            nc.sync.dma_start(out=res[:, i0:i1, :], in_=r_rows[:, i0:i1, :])
+
+        load_x(0)
+        for q in range(4):
+            nc.scalar.dma_start(
+                out=s8[32 * q : 32 * q + 12, :].bitcast(I32), in_=w8_scales[:, 4 * q : 4 * q + 4, :].bitcast(I32)
+            )
+        for q in range(4):
+            nc.gpsimd.dma_start(
+                out=s4[32 * q : 32 * q + 4, :, :].bitcast(I32),
+                in_=w4_scales[:, 4 * q : 4 * q + 4, :].bitcast(I32).rearrange("a r n -> r a n"),
+            )
+        nc.scalar.activation(out=junk[:], in_=one[:], func=ACT.Silu)
+        load_w8(0, 1, 0, C0)
+        load_w4(0, 1, 0, C0)
+        for a in range(1, NP):
+            load_x(a)
+            load_w8(a, a + 1, 0, C0)
+            load_w4(a, a + 1, 0, C0)
+        load_w4(0, NP, C0, M)
+        load_w8(0, NP, C0, 2 * C0)
+        load_r(0, 4)
+        load_w8(0, NP, 2 * C0, M)
+        load_r(4, 8)
+        load_r(8, 12)
+
+        def cast_x(a):
+            src = xf[a][:].rearrange("p j t -> p t j")
+            for t0, t1 in ((0, T // 2), (T // 2, SPLIT)):
+                nc.vector.tensor_copy(out=xb[a][:, t0:t1, :], in_=src[:, t0:t1, :])
+            nc.scalar.copy(out=xb[a][:, SPLIT:T, :], in_=src[:, SPLIT:T, :])
+
+        def quantize_x(a):
+            for t0 in (0, T // 2):
+                t1 = t0 + T // 2
+                nc.vector.quantize_mx(
+                    out=xc[:, a, t0:t1].bitcast(FP8X4),
+                    scales=xs[:, a, t0:t1],
+                    in_=xb[a][:, t0:t1, :].rearrange("p t j -> p (t j)"),
+                )
+
+        def gate(dst, i, a):
+            n0, n1 = i * P, (i + 1) * P
+            nc.tensor.matmul_mx(
+                out=dst,
+                lhsT=w4[:, a, 2 * n0 : 2 * n1].bitcast(FP4X4),
+                lhsT_scale=s4[:, a, n0:n1],
+                rhs=xc[:, a, :].bitcast(FP8X4),
+                rhs_scale=xs[:, a, :],
+                start=(a == 0),
+                stop=(a == NP - 1),
+            )
+
+        def up(dst, i, a, t0, t1):
+            n0, n1 = i * P, (i + 1) * P
+            nc.tensor.matmul_mx(
+                out=dst,
+                lhsT=w8[:, a, n0:n1].bitcast(FP8X4),
+                lhsT_scale=s8[4 * a : P, n0:n1],
+                rhs=xc[:, a, t0:t1].bitcast(FP8X4),
+                rhs_scale=xs[:, a, t0:t1],
+                start=(a == 0),
+                stop=(a == NP - 1),
+            )
+
+        def bank(kind, i):
+            return psum.tile([P, T], F32, name="%s%d" % (kind, i % 4))
+
+        g, u, act, y = {}, {}, {}, {}
+
+        def silu(i):
+            act[i] = work.tile([P, T], F32, name="act")
+            nc.scalar.activation(out=act[i][:], in_=g[i][:], func=ACT.Silu)
+
+        def mul(i):
+            y[i] = keep.tile([P, T], F32, name="y%d" % i, align_bytes=256)
+            nc.vector.tensor_tensor(out=y[i][:], in0=u[i][:], in1=act[i][:], op=ALU.mult)
+
+        def add_store(i):
+            nc.vector.tensor_tensor(out=y[i][:], in0=y[i][:], in1=res[:, i, :], op=ALU.add)
+            nc.sync.dma_start(out=out_rows[:, i, :], in_=y[i][:])
+
+        for i in range(4):
+            g[i] = bank("g", i)
+            u[i] = bank("u", i)
+        for a in range(NP):
+            cast_x(a)
+            quantize_x(a)
+            if a < NP - 1:
+                for i in range(4):
+                    up(u[i][:], i, a, 0, T)
+                for i in range(4):
+                    gate(g[i][:], i, a)
+            else:
+                for i in range(4):
+                    gate(g[i][:], i, a)
+                    up(u[i][:], i, a, 0, T)
+        for i in range(4):
+            silu(i)
+            mul(i)
+
+        adds = {4: (0, 1), 5: (2, 3), 6: (4, 5), 7: (6,), 8: (7,), 9: (8,), 10: (9, 10)}
+        for i in range(4, NT - 1):
+            g[i] = bank("g", i)
+            u[i] = bank("u", i)
+            for a in range(NP):
+                gate(g[i][:], i, a)
+            for a in range(NP):
+                up(u[i][:], i, a, 0, T)
+            silu(i)
+            mul(i)
+            for k in adds[i]:
+                add_store(k)
+
+        i = NT - 1
+        g[i] = bank("g", i)
+        for a in range(NP):
+            gate(g[i][:], i, a)
+        halves = ((0, T // 2), (T // 2, T))
+        ub = [bank("u", i), bank("u", 0)]
+        for h, (t0, t1) in enumerate(halves):
+            for a in range(NP):
+                up(ub[h][:, t0:t1], i, a, t0, t1)
+        silu(i)
+        y[i] = keep.tile([P, T], F32, name="ylast", align_bytes=256)
+        for h, (t0, t1) in enumerate(halves):
+            nc.vector.tensor_tensor(out=y[i][:, t0:t1], in0=ub[h][:, t0:t1], in1=act[i][:, t0:t1], op=ALU.mult)
+        for t0, t1 in halves:
+            nc.vector.tensor_tensor(out=y[i][:, t0:t1], in0=y[i][:, t0:t1], in1=res[:, i, t0:t1], op=ALU.add)
+            nc.sync.dma_start(out=out_rows[:, i, t0:t1], in_=y[i][:, t0:t1])

@@ -21,7 +21,7 @@ KP = P * PACK
 NP = K // KP
 NT = M // P
 C0 = 512
-SPLIT = 320
+SPLIT = 352
 
 
 def tile_mix_glu48_fm_res_kernel(tc, x, w4_words, w4_scales, w8_words, w8_scales, r, out):
@@ -36,8 +36,8 @@ def tile_mix_glu48_fm_res_kernel(tc, x, w4_words, w4_scales, w8_words, w8_scales
         psum = ctx.enter_context(tc.psum_pool(name="psum", bufs=1))
         ctx.enter_context(tc.manual_schedule())
 
-        w8 = keep.tile([P, NP, M], U32, name="w8", align_bytes=256)
-        w4 = keep.tile([P, NP, 2 * M], U8, name="w4", align_bytes=256)
+        w8 = {}
+        w4 = {}
         s8 = keep.tile([P, M], U8, name="s8", align_bytes=256)
         s4 = keep.tile([P, NP, M], U8, name="s4", align_bytes=256)
         xc = keep.tile([P, NP, T], U32, name="xc", align_bytes=256)
@@ -48,57 +48,68 @@ def tile_mix_glu48_fm_res_kernel(tc, x, w4_words, w4_scales, w8_words, w8_scales
         one = keep.tile([P, 1], F32, name="one")
         junk = keep.tile([P, 1], F32, name="junk")
 
-        nc.vector.memset(s8[:].bitcast(U32), 0)
         nc.vector.memset(s4[:].rearrange("p a n -> p (a n)").bitcast(U32), 0)
+        nc.vector.memset(s8[:].bitcast(U32), 0)
         nc.vector.memset(one[:], 0.0)
 
+        HALVES = ((0, T // 2), (T // 2, T))
+
         def load_x(a):
-            nc.sync.dma_start(out=xf[a][:], in_=x[a * KP : (a + 1) * KP, :].rearrange("(p j) t -> p j t", j=PACK))
+            rows = x[a * KP : (a + 1) * KP, :].rearrange("(p j) t -> p j t", j=PACK)
+            nc.sync.dma_start(out=xf[a][:], in_=rows)
 
-        def load_w8(a0, a1, c0, c1):
+        def load_w8(eng, a0, a1, c0, c1):
             for_a = w8_rows[a0:a1, :, 4 * c0 : 4 * c1].bitcast(I32).rearrange("a p n -> p a n")
-            nc.sync.dma_start(out=w8[:, a0:a1, c0:c1].bitcast(I32), in_=for_a)
+            t = keep.tile([P, a1 - a0, c1 - c0], U32, name="w8_%d_%d" % (a0, c0), align_bytes=256)
+            eng.dma_start(out=t[:].bitcast(I32), in_=for_a)
+            for a in range(a0, a1):
+                for n0 in range(c0, c1, P):
+                    w8[a, n0] = t[:, a - a0, n0 - c0 : n0 - c0 + P]
 
-        def load_w4(a0, a1, c0, c1):
+        def load_w4(eng, a0, a1, c0, c1):
             for_a = w4_words[a0:a1, :, 2 * c0 : 2 * c1].bitcast(I32).rearrange("a p n -> p a n")
-            nc.sync.dma_start(out=w4[:, a0:a1, 2 * c0 : 2 * c1].bitcast(I32), in_=for_a)
+            t = keep.tile([P, a1 - a0, 2 * (c1 - c0)], U8, name="w4_%d_%d" % (a0, c0), align_bytes=256)
+            eng.dma_start(out=t[:].bitcast(I32), in_=for_a)
+            for a in range(a0, a1):
+                for n0 in range(c0, c1, P):
+                    w4[a, n0] = t[:, a - a0, 2 * (n0 - c0) : 2 * (n0 - c0 + P)]
 
         def load_r(i0, i1):
             nc.sync.dma_start(out=res[:, i0:i1, :], in_=r_rows[:, i0:i1, :])
 
         load_x(0)
+        load_w8(nc.sync, 0, 1, 0, C0)
+        load_w4(nc.sync, 0, 1, 0, C0)
+        load_x(1)
         for q in range(4):
-            nc.scalar.dma_start(
-                out=s8[32 * q : 32 * q + 12, :].bitcast(I32), in_=w8_scales[:, 4 * q : 4 * q + 4, :].bitcast(I32)
-            )
-        for q in range(4):
-            nc.gpsimd.dma_start(
-                out=s4[32 * q : 32 * q + 4, :, :].bitcast(I32),
-                in_=w4_scales[:, 4 * q : 4 * q + 4, :].bitcast(I32).rearrange("a r n -> r a n"),
+            eng = nc.scalar if q < 2 else nc.sync
+            eng.dma_start(
+                out=s8[32 * q + 4 : 32 * q + 16, :].bitcast(I32), in_=w8_scales[:, 4 * q : 4 * q + 4, :].bitcast(I32)
             )
         nc.scalar.activation(out=junk[:], in_=one[:], func=ACT.Silu)
-        load_w8(0, 1, 0, C0)
-        load_w4(0, 1, 0, C0)
+        s4_rows = w4_scales.bitcast(I32).rearrange("a (q r) n -> r q a n", r=4)
+        for k in range(4):
+            nc.gpsimd.dma_start(out=s4[k:P:32, :, :].bitcast(I32), in_=s4_rows[k])
         for a in range(1, NP):
-            load_x(a)
-            load_w8(a, a + 1, 0, C0)
-            load_w4(a, a + 1, 0, C0)
-        load_w4(0, NP, C0, M)
-        load_w8(0, NP, C0, 2 * C0)
+            load_w8(nc.sync, a, a + 1, 0, C0)
+            load_w4(nc.sync, a, a + 1, 0, C0)
+            if a == 1:
+                load_x(2)
+        load_w4(nc.sync, 0, NP, C0, M)
+        load_w8(nc.sync, 0, NP, C0, 2 * C0)
         load_r(0, 4)
-        load_w8(0, NP, 2 * C0, M)
         load_r(4, 8)
+        load_w8(nc.sync, 0, NP, 2 * C0, M)
         load_r(8, 12)
 
         def cast_x(a):
             src = xf[a][:].rearrange("p j t -> p t j")
             for t0, t1 in ((0, T // 2), (T // 2, SPLIT)):
                 nc.vector.tensor_copy(out=xb[a][:, t0:t1, :], in_=src[:, t0:t1, :])
-            nc.scalar.copy(out=xb[a][:, SPLIT:T, :], in_=src[:, SPLIT:T, :])
+            nc.scalar.copy(out=xb[a][:, SPLIT:, :], in_=src[:, SPLIT:, :])
 
         def quantize_x(a):
-            for t0 in (0, T // 2):
-                t1 = t0 + T // 2
+            for t0, t1 in HALVES:
                 nc.vector.quantize_mx(
                     out=xc[:, a, t0:t1].bitcast(FP8X4),
                     scales=xs[:, a, t0:t1],
@@ -109,7 +120,7 @@ def tile_mix_glu48_fm_res_kernel(tc, x, w4_words, w4_scales, w8_words, w8_scales
             n0, n1 = i * P, (i + 1) * P
             nc.tensor.matmul_mx(
                 out=dst,
-                lhsT=w4[:, a, 2 * n0 : 2 * n1].bitcast(FP4X4),
+                lhsT=w4[a, n0].bitcast(FP4X4),
                 lhsT_scale=s4[:, a, n0:n1],
                 rhs=xc[:, a, :].bitcast(FP8X4),
                 rhs_scale=xs[:, a, :],
@@ -121,8 +132,8 @@ def tile_mix_glu48_fm_res_kernel(tc, x, w4_words, w4_scales, w8_words, w8_scales
             n0, n1 = i * P, (i + 1) * P
             nc.tensor.matmul_mx(
                 out=dst,
-                lhsT=w8[:, a, n0:n1].bitcast(FP8X4),
-                lhsT_scale=s8[4 * a : P, n0:n1],
+                lhsT=w8[a, n0].bitcast(FP8X4),
+                lhsT_scale=s8[4 * (a + 1) : P, n0:n1],
                 rhs=xc[:, a, t0:t1].bitcast(FP8X4),
                 rhs_scale=xs[:, a, t0:t1],
                 start=(a == 0),
@@ -165,7 +176,7 @@ def tile_mix_glu48_fm_res_kernel(tc, x, w4_words, w4_scales, w8_words, w8_scales
             silu(i)
             mul(i)
 
-        adds = {4: (0, 1), 5: (2, 3), 6: (4, 5), 7: (6,), 8: (7,), 9: (8,), 10: (9, 10)}
+        adds = {4: (0, 1), 5: (2, 3), 6: (4, 5), 7: (6, 7), 8: (8,), 9: (9,), 10: (10,)}
         for i in range(4, NT - 1):
             g[i] = bank("g", i)
             u[i] = bank("u", i)
@@ -182,15 +193,15 @@ def tile_mix_glu48_fm_res_kernel(tc, x, w4_words, w4_scales, w8_words, w8_scales
         g[i] = bank("g", i)
         for a in range(NP):
             gate(g[i][:], i, a)
-        halves = ((0, T // 2), (T // 2, T))
-        ub = [bank("u", i), bank("u", 0)]
-        for h, (t0, t1) in enumerate(halves):
+        pieces = ((0, 256), (256, 384), (384, 512))
+        ub = [bank("u", i), bank("u", 0), bank("u", 1)]
+        for (t0, t1), b in zip(pieces, ub):
             for a in range(NP):
-                up(ub[h][:, t0:t1], i, a, t0, t1)
+                up(b[:, t0:t1], i, a, t0, t1)
         silu(i)
         y[i] = keep.tile([P, T], F32, name="ylast", align_bytes=256)
-        for h, (t0, t1) in enumerate(halves):
-            nc.vector.tensor_tensor(out=y[i][:, t0:t1], in0=ub[h][:, t0:t1], in1=act[i][:, t0:t1], op=ALU.mult)
-        for t0, t1 in halves:
+        for (t0, t1), b in zip(pieces, ub):
+            nc.vector.tensor_tensor(out=y[i][:, t0:t1], in0=b[:, t0:t1], in1=act[i][:, t0:t1], op=ALU.mult)
             nc.vector.tensor_tensor(out=y[i][:, t0:t1], in0=y[i][:, t0:t1], in1=res[:, i, t0:t1], op=ALU.add)
+        for t0, t1 in HALVES:
             nc.sync.dma_start(out=out_rows[:, i, t0:t1], in_=y[i][:, t0:t1])

@@ -80,6 +80,7 @@ def tile_mix_glu48_fm_res_kernel(tc, x, w4_words, w4_scales, w8_words, w8_scales
         load_x(0)
         load_w8(nc.sync, 0, 1, 0, C0)
         load_w4(nc.sync, 0, 1, 0, C0)
+        load_w4(nc.sync, 1, 2, 0, C0)
         load_x(1)
         for q in range(4):
             eng = nc.scalar if q < 2 else nc.sync
@@ -90,13 +91,12 @@ def tile_mix_glu48_fm_res_kernel(tc, x, w4_words, w4_scales, w8_words, w8_scales
         s4_rows = w4_scales.bitcast(I32).rearrange("a (q r) n -> r q a n", r=4)
         for k in range(4):
             nc.gpsimd.dma_start(out=s4[k:P:32, :, :].bitcast(I32), in_=s4_rows[k])
-        for a in range(1, NP):
-            load_w8(nc.sync, a, a + 1, 0, C0)
-            load_w4(nc.sync, a, a + 1, 0, C0)
-            if a == 1:
-                load_x(2)
-        load_w4(nc.sync, 0, NP, C0, M)
+        load_x(2)
+        load_w8(nc.sync, 1, 2, 0, C0)
+        load_w4(nc.sync, 2, 3, 0, C0)
+        load_w8(nc.sync, 2, 3, 0, C0)
         load_w8(nc.sync, 0, NP, C0, 2 * C0)
+        load_w4(nc.sync, 0, NP, C0, M)
         load_r(0, 4)
         load_r(4, 8)
         load_w8(nc.sync, 0, NP, 2 * C0, M)
@@ -153,8 +153,10 @@ def tile_mix_glu48_fm_res_kernel(tc, x, w4_words, w4_scales, w8_words, w8_scales
             y[i] = keep.tile([P, T], F32, name="y%d" % i, align_bytes=256)
             nc.vector.tensor_tensor(out=y[i][:], in0=u[i][:], in1=act[i][:], op=ALU.mult)
 
-        def add_store(i):
-            nc.vector.tensor_tensor(out=y[i][:], in0=y[i][:], in1=res[:, i, :], op=ALU.add)
+        def add(eng, i):
+            eng.tensor_tensor(out=y[i][:], in0=y[i][:], in1=res[:, i, :], op=ALU.add)
+
+        def store(i):
             nc.sync.dma_start(out=out_rows[:, i, :], in_=y[i][:])
 
         for i in range(4):
@@ -163,11 +165,16 @@ def tile_mix_glu48_fm_res_kernel(tc, x, w4_words, w4_scales, w8_words, w8_scales
         for a in range(NP):
             cast_x(a)
             quantize_x(a)
-            if a < NP - 1:
+            if a == 0:
                 for i in range(4):
                     up(u[i][:], i, a, 0, T)
                 for i in range(4):
                     gate(g[i][:], i, a)
+            elif a == 1:
+                for i in range(4):
+                    gate(g[i][:], i, a)
+                for i in range(4):
+                    up(u[i][:], i, a, 0, T)
             else:
                 for i in range(4):
                     gate(g[i][:], i, a)
@@ -175,26 +182,35 @@ def tile_mix_glu48_fm_res_kernel(tc, x, w4_words, w4_scales, w8_words, w8_scales
         for i in range(4):
             silu(i)
             mul(i)
+            add(nc.gpsimd, i)
 
-        adds = {4: (0, 1), 5: (2, 3), 6: (4, 5), 7: (6, 7), 8: (8,), 9: (9,), 10: (10,)}
+        vadds = {6: 5, 7: 6, 8: 8, 9: 9}
         for i in range(4, NT - 1):
             g[i] = bank("g", i)
             u[i] = bank("u", i)
+            if i == 4:
+                for a in range(NP):
+                    up(u[i][:], i, a, 0, T)
             for a in range(NP):
                 gate(g[i][:], i, a)
-            for a in range(NP):
-                up(u[i][:], i, a, 0, T)
+            if i != 4:
+                for a in range(NP):
+                    up(u[i][:], i, a, 0, T)
             silu(i)
             mul(i)
-            for k in adds[i]:
-                add_store(k)
+            if i in (4, 7, 10):
+                add(nc.gpsimd, i)
+            if i in vadds:
+                add(nc.vector, vadds[i])
+        for i in (0, 1, 5, 2, 6, 3, 4, 8, 7, 9):
+            store(i)
 
         i = NT - 1
         g[i] = bank("g", i)
         for a in range(NP):
             gate(g[i][:], i, a)
-        pieces = ((0, 256), (256, 384), (384, 512))
-        ub = [bank("u", i), bank("u", 0), bank("u", 1)]
+        pieces = HALVES
+        ub = [bank("u", i), bank("u", 0)]
         for (t0, t1), b in zip(pieces, ub):
             for a in range(NP):
                 up(b[:, t0:t1], i, a, t0, t1)
@@ -202,6 +218,7 @@ def tile_mix_glu48_fm_res_kernel(tc, x, w4_words, w4_scales, w8_words, w8_scales
         y[i] = keep.tile([P, T], F32, name="ylast", align_bytes=256)
         for (t0, t1), b in zip(pieces, ub):
             nc.vector.tensor_tensor(out=y[i][:, t0:t1], in0=b[:, t0:t1], in1=act[i][:, t0:t1], op=ALU.mult)
-            nc.vector.tensor_tensor(out=y[i][:, t0:t1], in0=y[i][:, t0:t1], in1=res[:, i, t0:t1], op=ALU.add)
+        store(NT - 2)
         for t0, t1 in HALVES:
+            nc.vector.tensor_tensor(out=y[i][:, t0:t1], in0=y[i][:, t0:t1], in1=res[:, i, t0:t1], op=ALU.add)
             nc.sync.dma_start(out=out_rows[:, i, t0:t1], in_=y[i][:, t0:t1])

from contextlib import ExitStack

import concourse.mybir as mybir

K, M, T = 1536, 1536, 512
FLOPS = 2 * 2 * K * M * T

F32 = mybir.dt.float32
BF16 = mybir.dt.bfloat16
I32 = mybir.dt.int32
U32 = mybir.dt.uint32
U8 = mybir.dt.uint8
FP8X4 = mybir.dt.float8_e4m3fn_x4
FP4X4 = mybir.dt.float4_e2m1fn_x4
ACT = mybir.ActivationFunctionType
ALU = mybir.AluOpType

P = 128
PACK = 4
KP = P * PACK
NP = K // KP
NT = M // P
C0 = 512
SPLIT = 352


def tile_mix_glu48_fm_res_kernel(tc, x, w4_words, w4_scales, w8_words, w8_scales, r, out):
    nc = tc.nc
    w8_rows = w8_words.rearrange("a p n i -> a p (n i)")
    r_rows = r.rearrange("(i p) t -> p i t", p=P)
    out_rows = out.rearrange("(i p) t -> p i t", p=P)

    with ExitStack() as ctx:
        keep = ctx.enter_context(tc.tile_pool(name="keep", bufs=1))
        work = ctx.enter_context(tc.tile_pool(name="work", bufs=4))
        psum = ctx.enter_context(tc.psum_pool(name="psum", bufs=1))
        ctx.enter_context(tc.manual_schedule())

        w8 = {}
        w4 = {}
        s8 = keep.tile([P, M], U8, name="s8", align_bytes=256)
        s4 = keep.tile([P, NP, M], U8, name="s4", align_bytes=256)
        xc = keep.tile([P, NP, T], U32, name="xc", align_bytes=256)
        xs = keep.tile([P, NP, T], U8, name="xs", align_bytes=256)
        res = keep.tile([P, NT, T], F32, name="res", align_bytes=256)
        xf = [keep.tile([P, PACK, T], F32, name="xf%d" % a, align_bytes=256) for a in range(NP)]
        xb = [keep.tile([P, T, PACK], BF16, name="xb%d" % a, align_bytes=256) for a in range(NP)]
        one = keep.tile([P, 1], F32, name="one")
        junk = keep.tile([P, 1], F32, name="junk")

        nc.vector.memset(s4[:].rearrange("p a n -> p (a n)").bitcast(U32), 0)
        nc.vector.memset(s8[:].bitcast(U32), 0)
        nc.vector.memset(one[:], 0.0)

        HALVES = ((0, T // 2), (T // 2, T))

        def load_x(a):
            rows = x[a * KP : (a + 1) * KP, :].rearrange("(p j) t -> p j t", j=PACK)
            nc.sync.dma_start(out=xf[a][:], in_=rows)

        def load_w8(eng, a0, a1, c0, c1):
            for_a = w8_rows[a0:a1, :, 4 * c0 : 4 * c1].bitcast(I32).rearrange("a p n -> p a n")
            t = keep.tile([P, a1 - a0, c1 - c0], U32, name="w8_%d_%d" % (a0, c0), align_bytes=256)
            eng.dma_start(out=t[:].bitcast(I32), in_=for_a)
            for a in range(a0, a1):
                for n0 in range(c0, c1, P):
                    w8[a, n0] = t[:, a - a0, n0 - c0 : n0 - c0 + P]

        def load_w4(eng, a0, a1, c0, c1):
            for_a = w4_words[a0:a1, :, 2 * c0 : 2 * c1].bitcast(I32).rearrange("a p n -> p a n")
            t = keep.tile([P, a1 - a0, 2 * (c1 - c0)], U8, name="w4_%d_%d" % (a0, c0), align_bytes=256)
            eng.dma_start(out=t[:].bitcast(I32), in_=for_a)
            for a in range(a0, a1):
                for n0 in range(c0, c1, P):
                    w4[a, n0] = t[:, a - a0, 2 * (n0 - c0) : 2 * (n0 - c0 + P)]

        def load_r(i0, i1):
            nc.sync.dma_start(out=res[:, i0:i1, :], in_=r_rows[:, i0:i1, :])

        load_x(0)
        load_w8(nc.sync, 0, 1, 0, C0)
        load_w4(nc.sync, 0, 1, 0, C0)
        load_w4(nc.sync, 1, 2, 0, C0)
        load_x(1)
        for q in range(4):
            eng = nc.scalar if q < 2 else nc.sync
            eng.dma_start(
                out=s8[32 * q + 4 : 32 * q + 16, :].bitcast(I32), in_=w8_scales[:, 4 * q : 4 * q + 4, :].bitcast(I32)
            )
        nc.scalar.activation(out=junk[:], in_=one[:], func=ACT.Silu)
        s4_rows = w4_scales.bitcast(I32).rearrange("a (q r) n -> r q a n", r=4)
        for k in range(4):
            nc.gpsimd.dma_start(out=s4[k:P:32, :, :].bitcast(I32), in_=s4_rows[k])
        load_x(2)
        load_w8(nc.sync, 1, 2, 0, C0)
        load_w4(nc.sync, 2, 3, 0, C0)
        load_w8(nc.sync, 2, 3, 0, C0)
        load_w8(nc.sync, 0, NP, C0, 2 * C0)
        load_w4(nc.sync, 0, NP, C0, M)
        load_r(0, 4)
        load_r(4, 8)
        load_w8(nc.sync, 0, NP, 2 * C0, M)
        load_r(8, 12)

        def cast_x(a):
            src = xf[a][:].rearrange("p j t -> p t j")
            for t0, t1 in ((0, T // 2), (T // 2, SPLIT)):
                nc.vector.tensor_copy(out=xb[a][:, t0:t1, :], in_=src[:, t0:t1, :])
            nc.scalar.copy(out=xb[a][:, SPLIT:, :], in_=src[:, SPLIT:, :])

        def quantize_x(a):
            for t0, t1 in HALVES:
                nc.vector.quantize_mx(
                    out=xc[:, a, t0:t1].bitcast(FP8X4),
                    scales=xs[:, a, t0:t1],
                    in_=xb[a][:, t0:t1, :].rearrange("p t j -> p (t j)"),
                )

        def gate(dst, i, a):
            n0, n1 = i * P, (i + 1) * P
            nc.tensor.matmul_mx(
                out=dst,
                lhsT=w4[a, n0].bitcast(FP4X4),
                lhsT_scale=s4[:, a, n0:n1],
                rhs=xc[:, a, :].bitcast(FP8X4),
                rhs_scale=xs[:, a, :],
                start=(a == 0),
                stop=(a == NP - 1),
            )

        def up(dst, i, a, t0, t1):
            n0, n1 = i * P, (i + 1) * P
            nc.tensor.matmul_mx(
                out=dst,
                lhsT=w8[a, n0].bitcast(FP8X4),
                lhsT_scale=s8[4 * (a + 1) : P, n0:n1],
                rhs=xc[:, a, t0:t1].bitcast(FP8X4),
                rhs_scale=xs[:, a, t0:t1],
                start=(a == 0),
                stop=(a == NP - 1),
            )

        def bank(kind, i):
            return psum.tile([P, T], F32, name="%s%d" % (kind, i % 4))

        g, u, act, y = {}, {}, {}, {}

        def silu(i):
            act[i] = work.tile([P, T], F32, name="act")
            nc.scalar.activation(out=act[i][:], in_=g[i][:], func=ACT.Silu)

        def mul(i):
            y[i] = keep.tile([P, T], F32, name="y%d" % i, align_bytes=256)
            nc.vector.tensor_tensor(out=y[i][:], in0=u[i][:], in1=act[i][:], op=ALU.mult)

        def add(eng, i):
            eng.tensor_tensor(out=y[i][:], in0=y[i][:], in1=res[:, i, :], op=ALU.add)

        def store(i):
            nc.sync.dma_start(out=out_rows[:, i, :], in_=y[i][:])

        for i in range(4):
            g[i] = bank("g", i)
            u[i] = bank("u", i)
        for a in range(NP):
            cast_x(a)
            quantize_x(a)
            if a == 0:
                for i in range(4):
                    up(u[i][:], i, a, 0, T)
                for i in range(4):
                    gate(g[i][:], i, a)
            elif a == 1:
                for i in range(4):
                    gate(g[i][:], i, a)
                for i in range(4):
                    up(u[i][:], i, a, 0, T)
            else:
                for i in range(4):
                    gate(g[i][:], i, a)
                    up(u[i][:], i, a, 0, T)
        for i in range(4):
            silu(i)
            mul(i)
            add(nc.gpsimd, i)

        vadds = {6: 5, 7: 6, 8: 8, 9: 9}
        for i in range(4, NT - 1):
            g[i] = bank("g", i)
            u[i] = bank("u", i)
            if i == 4:
                for a in range(NP):
                    up(u[i][:], i, a, 0, T)
            for a in range(NP):
                gate(g[i][:], i, a)
            if i != 4:
                for a in range(NP):
                    up(u[i][:], i, a, 0, T)
            silu(i)
            mul(i)
            if i in (4, 7, 10):
                add(nc.gpsimd, i)
            if i in vadds:
                add(nc.vector, vadds[i])
        for i in (0, 1, 5, 2, 6, 3, 4, 8, 7, 9):
            store(i)

        i = NT - 1
        g[i] = bank("g", i)
        for a in range(NP):
            gate(g[i][:], i, a)
        pieces = HALVES
        ub = [bank("u", i), bank("u", 0)]
        for (t0, t1), b in zip(pieces, ub):
            for a in range(NP):
                up(b[:, t0:t1], i, a, t0, t1)
        silu(i)
        y[i] = keep.tile([P, T], F32, name="ylast", align_bytes=256)
        for (t0, t1), b in zip(pieces, ub):
            nc.vector.tensor_tensor(out=y[i][:, t0:t1], in0=b[:, t0:t1], in1=act[i][:, t0:t1], op=ALU.mult)
        store(NT - 2)
        for t0, t1 in HALVES:
            nc.vector.tensor_tensor(out=y[i][:, t0:t1], in0=y[i][:, t0:t1], in1=res[:, i, t0:t1], op=ALU.add)
            nc.sync.dma_start(out=out_rows[:, i, t0:t1], in_=y[i][:, t0:t1])
